import numpy as np
import ml_dtypes


def mxq(x, axis, fmt="e4m3"):
    dtype, down = {"e4m3": (ml_dtypes.float8_e4m3fn, 7), "e5m2": (ml_dtypes.float8_e5m2, 14)}[fmt]
    v = np.moveaxis(np.asarray(x, np.float32).astype(ml_dtypes.bfloat16).astype(np.float64), axis, -1)
    blocks = v.reshape(v.shape[:-1] + (-1, 32))
    amax = np.abs(blocks).max(-1, keepdims=True)
    byte = np.maximum(np.where(amax > 0, np.frexp(amax)[1] - 1 + 127, 0) - down, 1)
    scale = np.exp2(byte - 127.0)
    codes = (blocks / scale).astype(np.float32).astype(dtype).astype(np.float64)
    return np.moveaxis((codes * scale).reshape(v.shape), -1, axis)


WIDE = False


def mx_kscale(k):
    if not WIDE:
        return np.ones(k)
    levels = np.array([10, -10, 5, -5, 0])
    if k % 512:
        return np.exp2(np.random.permutation(np.resize(levels, k // 32))).repeat(32)
    a = np.empty((k // 512, 16))
    for p in range(k // 512):
        a[p, :8] = np.random.permutation(np.resize(levels, 8))
        for g in range(8):
            far = levels[np.abs(levels - a[p, g]) >= 10]
            a[p, g + 8] = far[np.random.randint(len(far))]
    return np.exp2(a.ravel()).repeat(32)


def f64(x):
    return np.asarray(x).astype(np.float64)


def striped(idx):
    return np.tile(np.asarray(idx).reshape(-1, 16).T, (8, 1)).astype(np.uint16)


def unstriped(offs):
    return offs[:16].T.reshape(-1).astype(np.int64)


E2M1 = np.array([0.0, 0.5, 1.0, 1.5, 2.0, 3.0, 4.0, 6.0, -0.0, -0.5, -1.0, -1.5, -2.0, -3.0, -4.0, -6.0])


def pack_weight(w, fmt):
    k, n = w.shape
    w = f64(np.asarray(w, np.float32).astype(ml_dtypes.bfloat16)).reshape(k // 32, 32, n)
    amax = np.abs(w).max(1)
    if fmt == "e4m3":
        byte = np.frexp(amax)[1] - 1 + 127 - 7
    else:
        mant, ex = np.frexp(amax / 6.0)
        byte = np.where(mant > 0.5, ex, ex - 1) + 127
    byte = np.clip(np.where(amax > 0, byte, 1), 1, 254)
    scaled = (w * np.exp2(127.0 - byte)[:, None, :]).reshape(k, n).astype(np.float32)
    by_word = np.ascontiguousarray(scaled.reshape(k // 512, 128, 4, n).transpose(0, 1, 3, 2))
    if fmt == "e4m3":
        words = by_word.astype(ml_dtypes.float8_e4m3fn).view(np.uint8)
    else:
        c = by_word.astype(ml_dtypes.float4_e2m1fn).view(np.uint8) & 0xF
        words = (c[..., 0::2] | (c[..., 1::2] << 4)).reshape(k // 512, 128, 2 * n)
    return np.ascontiguousarray(words), np.ascontiguousarray(byte.astype(np.uint8).reshape(k // 512, 16, n))


def unpack_weight(words, scales, fmt):
    g, _, n = scales.shape
    words = np.ascontiguousarray(words).reshape(g, 128, n, -1)
    if fmt == "e4m3":
        vals = words.view(ml_dtypes.float8_e4m3fn).astype(np.float64)
    else:
        nib = np.empty((g, 128, n, 4), np.uint8)
        nib[..., 0::2] = words & 0xF
        nib[..., 1::2] = words >> 4
        vals = E2M1[nib]
    vals = vals * np.repeat(np.exp2(scales.astype(np.float64) - 127.0), 8, axis=1)[..., None]
    return vals.transpose(0, 1, 3, 2).reshape(g * 512, n)


def softplus(v):
    return np.log(1.0 + np.exp(v))


def sigmoid(v):
    return 1.0 / (1.0 + np.exp(-v))


D, T, I, Q, E, M = 512, 2048, 512, 256, 512, 1024


def setup_inputs():
    n = np.random.standard_normal
    idx = np.random.permutation(T)[:I]
    idx2 = np.random.permutation(M)[:Q]
    fd = mx_kscale(D)
    fi = mx_kscale(I)
    ti = np.ones(T)
    ti[idx] = fi
    keysp = pack_weight(n((D, T)) / fd[:, None], "e2m1")
    return {
        "query": (n((D, Q)) * 1.0 / np.sqrt(D) * fd[:, None]).astype(np.float32),
        "keys_words": keysp[0],
        "keys_scales": keysp[1],
        "ceil_t": np.tile(np.random.uniform(1.0, 4.0, T), (128, 1)).astype(np.float32),
        "halfp": np.tile(np.random.uniform(0.4, 1.5, T), (128, 1)).astype(np.float32),
        "eager": (np.random.uniform(0.8, 2.0, (Q, 1))).astype(np.float32),
        "thresh": (np.random.uniform(1.5, 4.0, (Q, 1))).astype(np.float32),
        "os": (np.random.uniform(4.0, 16.0, (1, I)) * fi).astype(np.float32),
        "vals": (n((E, T)) / ti).astype(np.float32),
        "old": (n((E, M)) * 2.0).astype(np.float32),
        "fade": (np.random.uniform(0.3, 0.9, (1, M))).astype(np.float32),
        "offs": striped(idx),
        "offs2": striped(idx2),
    }


def reference(query, keys_words, keys_scales, ceil_t, halfp, eager, thresh, os, vals, old, fade, offs, offs2):
    idx = unstriped(offs)
    idx2 = unstriped(offs2)
    keysu = unpack_weight(keys_words, keys_scales, "e2m1")
    queryq = mxq(f64(query), 0, "e4m3")
    keysidxg = keysu[:, idx]
    a = queryq.T @ keysidxg
    fa = softplus(a * 2.0)
    s = fa * f64(ceil_t)[:1][:, idx] / (fa + f64(halfp)[:1][:, idx])
    m0 = np.max(s, axis=1, keepdims=True)
    m1 = np.mean(s, axis=1, keepdims=True)
    p = np.exp(s - m0)
    gt0 = sigmoid((m0 - m1) * f64(eager) - f64(thresh))
    w = p / np.sum(p, axis=1, keepdims=True) * gt0
    wo1 = w * f64(os)
    wt1 = wo1.T
    vt1 = f64(vals)[:, idx].T
    vt1q = mxq(vt1, 0, "e4m3")
    wt1q = mxq(wt1, 0, "e4m3")
    o = vt1q.T @ wt1q
    of = np.zeros((E, M))
    of[:, idx2] = o
    y = f64(old) * f64(fade) + of
    return y

from contextlib import ExitStack

import concourse.mybir as mybir
from concourse.masks import make_identity

D, T, I, Q, E, M = 512, 2048, 512, 256, 512, 1024
FLOPS = 2 * D * Q * I + 2 * I * E * Q

F32 = mybir.dt.float32
BF16 = mybir.dt.bfloat16
I32 = mybir.dt.int32
U32 = mybir.dt.uint32
U16 = mybir.dt.uint16
U8 = mybir.dt.uint8
FP8X4 = mybir.dt.float8_e4m3fn_x4
FP4X4 = mybir.dt.float4_e2m1fn_x4
ACT = mybir.ActivationFunctionType
ALU = mybir.AluOpType
AXIS_X = mybir.AxisListType.X

P = 128
PACK = 4
R = I // P
QT = Q // P
ET = E // P
EXP_CAP = 2.0 ** 60

VALS_ON_SCALAR = (3,)
GP_COLS = 256


def tile_attend_saturating_abstaining_written_kernel(
    tc, query, keys_words, keys_scales, ceil_t, halfp, eager, thresh, slot_factor, vals, old, fade, offs, offs2, out
):
    nc = tc.nc
    with ExitStack() as ctx:
        lists = ctx.enter_context(tc.tile_pool(name="lists", bufs=1))
        sb = ctx.enter_context(tc.tile_pool(name="sb", bufs=1))
        ps = ctx.enter_context(tc.psum_pool(name="ps", bufs=1))

        def spread(bank_cols, column, start=True, stop=True):
            nc.tensor.matmul(bank_cols, lhsT=column.to_broadcast([P, P]), rhs=ident[:], start=start, stop=stop, is_transpose=True)

        def turn(bank_cols, block, start=True, stop=True):
            nc.tensor.matmul(bank_cols, lhsT=block, rhs=ident[:], start=start, stop=stop, is_transpose=True)

        slots = lists.tile([P, I // 16], U16, name="slots")
        places = lists.tile([P, Q // 16], U16, name="places")
        nc.sync.dma_start(slots[:], offs)
        nc.sync.dma_start(places[:], offs2)
        fade_cols = sb.tile([P, 2, 4], F32, name="fade_cols")
        nc.sync.dma_start(fade_cols[:], fade.rearrange("o (b p j) -> p (o b) j", b=2, j=4))
        q_raw = sb.tile([P, PACK, Q], F32, name="q_raw")
        nc.sync.dma_start(q_raw[:], query.rearrange("(p j) q -> p j q", j=PACK))
        kw_win = sb.tile([P, T], U16, name="kw_win", tag="w1", align_bytes=64)
        nc.sync.dma_start(kw_win[:].bitcast(I32), keys_words[0].bitcast(I32))
        vals_first = sb.tile([P, T], F32, name="vals_win0")
        nc.sync.dma_start(vals_first[:], vals[0:P, :])
        ks = sb.tile([P, I], U8, name="ks", align_bytes=64)
        ceil_win = sb.tile([P, T], F32, name="ceil_win", tag="w2", align_bytes=64)
        half_win = sb.tile([P, T], F32, name="half_win", tag="w3", align_bytes=64)
        with tc.tile_pool(name="head", bufs=1) as head:
            ks_win = head.tile([P, T], U8, name="ks_win", align_bytes=64)
            nc.vector.memset(ks_win[:].bitcast(I32), 0)
            for quad in range(4):
                nc.scalar.dma_start(
                    ks_win[32 * quad : 32 * quad + 4, :].bitcast(I32), keys_scales[0, 4 * quad : 4 * quad + 4, :].bitcast(I32)
                )
            nc.vector.memset(ceil_win[:].bitcast(I32), 0)
            nc.vector.memset(half_win[:].bitcast(I32), 0)
            nc.scalar.dma_start(ceil_win[0:1, :], ceil_t[0:1, :])
            nc.sync.dma_start(half_win[1:2, :], halfp[1:2, :])
            nc.vector.tensor_copy(ks[:], ks_win[:].indirect(slots[:]))

        late = ctx.enter_context(tc.tile_pool(name="late", bufs=1))
        factor_cols = late.tile([P, 4], F32, name="factor_cols")
        eager_cols = late.tile([P, QT], F32, name="eager_cols")
        thresh_cols = late.tile([P, QT], F32, name="thresh_cols")
        vals_win = [vals_first] + [late.tile([P, T], F32, name="vals_win%d" % e, tag="vals%d" % e) for e in range(1, ET)]
        old_sb = [late.tile([P, M], F32, name="old%d" % e) for e in range(ET)]
        for kind, e in (("v", 1), ("o", 0), ("o", 1), ("v", 2), ("o", 2), ("v", 3), ("o", 3)):
            if kind == "v":
                nc.sync.dma_start(vals_win[e][:], vals[e * P : (e + 1) * P, :])
            else:
                nc.sync.dma_start(old_sb[e][:], old[e * P : (e + 1) * P, :])
            if (kind, e) == ("o", 0):
                nc.sync.dma_start(factor_cols[:], slot_factor.rearrange("o (p j) -> p (o j)", j=4))
                with nc.allow_non_contiguous_dma(reason="one number a partition"):
                    nc.sync.dma_start(eager_cols[:], eager.rearrange("(t p) o -> p (t o)", p=P))
                    nc.sync.dma_start(thresh_cols[:], thresh.rearrange("(t p) o -> p (t o)", p=P))

        ident = sb.tile([P, P], F32, name="ident")
        make_identity(nc, ident[:])

        fade_rows = sb.tile([P, M], F32, name="fade_rows")
        for b in range(2):
            bank = ps.tile([P, 4, P], F32, name="fade_bank%d" % b, tag="a%d" % b)
            for j in range(4):
                spread(bank[:, j, :], fade_cols[:, b, j : j + 1])
            nc.scalar.activation(
                fade_rows[:, b * 512 : (b + 1) * 512].rearrange("p (k j) -> p k j", j=4), bank[:].rearrange("p j k -> p k j"), ACT.Copy
            )

        q_bf = sb.tile([P, Q, PACK], BF16, name="q_bf", tag="w0", align_bytes=64)
        nc.vector.tensor_copy(q_bf[:], q_raw[:].rearrange("p j q -> p q j"))
        kw = [sb.tile([P, I // 2], U16, name="kw%d" % h, align_bytes=64) for h in range(2)]
        nc.vector.tensor_copy(kw[0][:], kw_win[:].indirect(slots[:, 0:16]))
        q_codes = sb.tile([P, Q], U32, name="q_codes", align_bytes=64)
        q_scales = sb.tile([P, Q], U8, name="q_scales", align_bytes=64)
        nc.vector.quantize_mx(out=q_codes[:].bitcast(FP8X4), scales=q_scales[:], in_=q_bf[:].rearrange("p q j -> p (q j)"))
        nc.vector.tensor_copy(kw[1][:], kw_win[:].indirect(slots[:, 16:32]))

        scores = []
        for h in range(2):
            bank = ps.tile([P, 2, Q], F32, name="scores%d" % h, tag="a%d" % h)
            for rr in range(2):
                r = 2 * h + rr
                nc.tensor.matmul_mx(
                    out=bank[:, rr, :],
                    lhsT=kw[h][:, rr * P : (rr + 1) * P].bitcast(FP4X4),
                    lhsT_scale=ks[:, r * P : (r + 1) * P],
                    rhs=q_codes[:].bitcast(FP8X4),
                    rhs_scale=q_scales[:],
                    start=True,
                    stop=True,
                )
            scores.append(bank)

        ceil_g = sb.tile([P, I], F32, name="ceil_g")
        half_g = sb.tile([P, I], F32, name="half_g")
        nc.scalar.activation(ceil_g[:], ceil_win[:].indirect(slots[:]), ACT.Copy)
        grown = sb.tile([P, R, Q], F32, name="grown", tag="w2", align_bytes=64)
        capped = sb.tile([P, R, Q], F32, name="capped")
        soft = sb.tile([P, R, Q], F32, name="soft", tag="g1")
        for h in range(2):
            nc.scalar.activation(grown[:, 2 * h : 2 * h + 2, :], scores[h][:], ACT.Exp, scale=2.0)
        for h in range(2):
            nc.vector.tensor_scalar(capped[:, 2 * h : 2 * h + 2, :], grown[:, 2 * h : 2 * h + 2, :], EXP_CAP, 1.0, ALU.min, ALU.add)
        for h in range(2):
            nc.scalar.activation(soft[:, 2 * h : 2 * h + 2, :], capped[:, 2 * h : 2 * h + 2, :], ACT.Ln)

        nc.vector.tensor_copy(half_g[:], half_win[:].indirect(slots[:]))
        ch_bank = ps.tile([P, R, P], F32, name="ch_bank", tag="x")
        for r in range(R):
            turn(ch_bank[:, r, :], ceil_g[:, r * P : (r + 1) * P], True, False)
            turn(ch_bank[:, r, :], half_g[:, r * P : (r + 1) * P], False, True)
        ch = sb.tile([P, 2, R], F32, name="ch")
        nc.vector.tensor_copy(ch[:], ch_bank[:, :, 0:2].rearrange("p r c -> p c r"))
        ch_prod = sb.tile([P, R], F32, name="ch_prod")
        nc.vector.scalar_tensor_tensor(ch_prod[:], ch[:, 0, :], -1.0, ch[:, 1, :], ALU.mult, ALU.mult)
        ceil_sum = sb.tile([P, 1], F32, name="ceil_sum")
        nc.vector.tensor_reduce(ceil_sum[:], ch[:, 0, :], AXIS_X, ALU.add)

        v_codes, v_scales = [], []

        def prepare_values(e):
            v_bf = sb.tile([P, I], BF16, name="v_bf%d" % e, tag="g%d" % e)
            if e in VALS_ON_SCALAR:
                nc.scalar.activation(v_bf[:], vals_win[e][:].indirect(slots[:]), ACT.Copy)
            else:
                nc.vector.tensor_copy(v_bf[:], vals_win[e][:].indirect(slots[:]))
            v_bank = ps.tile([P, 2, P], F32, name="v_bank%d" % e, tag="v%d" % (e % 2))
            words = v_bf[:].bitcast(F32)
            for u in range(2):
                turn(v_bank[:, u, :], words[:, u : I // 2 : 2])
            v_in = sb.tile([P, P * PACK], BF16, name="v_in%d" % e, tag="in%d" % e, align_bytes=64)
            v_words = v_in[:].bitcast(F32).rearrange("p (q u) -> p q u", u=2)
            if e in VALS_ON_SCALAR:
                nc.scalar.copy(v_words, v_bank[:].rearrange("p u q -> p q u"))
            else:
                nc.vector.tensor_copy(v_words, v_bank[:].rearrange("p u q -> p q u"))
            codes = sb.tile([P, P], U32, name="v_codes%d" % e, align_bytes=64)
            scales = sb.tile([P, P], U8, name="v_scales%d" % e, align_bytes=64)
            nc.vector.quantize_mx(out=codes[:].bitcast(FP8X4), scales=scales[:], in_=v_in[:])
            v_codes.append(codes)
            v_scales.append(scales)

        prepare_values(0)

        fa = sb.tile([P, R, Q], F32, name="fa", tag="in0", align_bytes=64)
        for h in range(2):
            nc.vector.scalar_tensor_tensor(
                fa[:, 2 * h : 2 * h + 2, :], scores[h][:], 2.0, soft[:, 2 * h : 2 * h + 2, :], ALU.mult, ALU.max
            )
        absden = sb.tile([P, R, Q], F32, name="absden", tag="g2")
        for r in range(R):
            nc.scalar.activation(absden[:, r, :], fa[:, r, :], ACT.Abs, bias=ch[:, 1, r : r + 1])
        lnden = sb.tile([P, R, Q], F32, name="lnden", tag="g3")
        for h in range(2):
            nc.scalar.activation(lnden[:, 2 * h : 2 * h + 2, :], absden[:, 2 * h : 2 * h + 2, :], ACT.Ln)
        numer = sb.tile([P, R, Q], F32, name="numer", tag="k3")
        for r in range(R):
            nc.vector.tensor_scalar(
                numer[:, r, :], fa[:, r, :], ch[:, 1, r : r + 1], ch_prod[:, r : r + 1], ALU.add, ALU.mult
            )

        factor_bank = ps.tile([P, 4, P], F32, name="factor_bank", tag="os")
        for j in range(4):
            spread(factor_bank[:, j, :], factor_cols[:, j : j + 1])

        prepare_values(1)
        prepare_values(2)

        s_banks, sum_banks = [], []
        for t in range(QT):
            s_bank = ps.tile([P, I], F32, name="s_bank%d" % t, tag="a%d" % t)
            for r in range(R):
                spread(s_bank[:, r * P : (r + 1) * P], ch[:, 0, r : r + 1], r == 0, False)
            s_banks.append(s_bank)
            sum_bank = ps.tile([P, P], F32, name="sum_bank%d" % t, tag="f%d" % t)
            spread(sum_bank[:], ceil_sum[:, 0:1], True, False)
            sum_banks.append(sum_bank)

        inv2 = [sb.tile([P, R, P], F32, name="inv2_%d" % t) for t in range(QT)]
        for t in range(QT):
            nc.scalar.activation(inv2[t][:], lnden[:, :, t * P : (t + 1) * P], ACT.Exp, scale=-2.0)

        prepare_values(3)

        shorts = sb.tile([P, QT, R, P], F32, name="shorts", tag="in2", align_bytes=64)
        shares = sb.tile([P, QT, I], F32, name="shares", tag="g3")
        w_codes, w_scales = [], []
        for t in range(QT):
            short = shorts[:, t, :, :]
            nc.vector.tensor_tensor(short, numer[:, :, t * P : (t + 1) * P], inv2[t][:], ALU.mult)
            for r in range(R):
                turn(s_banks[t][:, r * P : (r + 1) * P], short[:, r, :], False, r == R - 1)
            sum_bank = sum_banks[t]
            for r in range(R):
                turn(sum_bank[:], short[:, r, :], False, r == R - 1)
            neg_max = sb.tile([P, 1], F32, name="neg_max%d" % t)
            nc.vector.tensor_reduce(neg_max[:], s_banks[t][:], AXIS_X, ALU.max, negate=True)
            p_sum = sb.tile([P, 1], F32, name="p_sum%d" % t)
            nc.scalar.activation(shares[:, t, :], s_banks[t][:], ACT.Exp, bias=neg_max[:], accum_out=p_sum[:])
            s_sum = sb.tile([P, 1], F32, name="s_sum%d" % t)
            nc.vector.tensor_reduce(s_sum[:], sum_bank[:], AXIS_X, ALU.add)
            gap = sb.tile([P, 1], F32, name="gap%d" % t)
            nc.vector.tensor_scalar(gap[:], s_sum[:], 1.0 / I, neg_max[:], ALU.mult, ALU.add)
            odds = late.tile([P, 1], F32, name="odds%d" % t, tag="vals3")
            nc.scalar.activation(odds[:], gap[:], ACT.Exp, bias=thresh_cols[:, t : t + 1], scale=eager_cols[:, t : t + 1])
            denom = sb.tile([P, 1], F32, name="denom%d" % t)
            nc.vector.tensor_scalar(denom[:], odds[:], 1.0, p_sum[:], ALU.add, ALU.mult)
            row = sb.tile([P, 1], F32, name="row%d" % t)
            nc.vector.reciprocal(row[:], denom[:])
            w_bf = sb.tile([P, I], BF16, name="w_bf%d" % t)
            nc.vector.scalar_tensor_tensor(
                w_bf[:].rearrange("p (k j) -> p k j", j=4),
                shares[:, t, :].rearrange("p (k j) -> p k j", j=4),
                row[:],
                factor_bank[:].rearrange("p j k -> p k j"),
                ALU.mult,
                ALU.mult,
            )
            w_bank = ps.tile([P, 2, P], F32, name="w_bank%d" % t, tag="v%d" % (1 - t))
            words = w_bf[:].bitcast(F32)
            for u in range(2):
                turn(w_bank[:, u, :], words[:, u : I // 2 : 2])
            w_in = sb.tile([P, P * PACK], BF16, name="w_in%d" % t, tag="in%d" % (3 + t), align_bytes=64)
            nc.scalar.copy(w_in[:].bitcast(F32).rearrange("p (q u) -> p q u", u=2), w_bank[:].rearrange("p u q -> p q u"))
            codes = sb.tile([P, P], U32, name="w_codes%d" % t, align_bytes=64)
            scales = sb.tile([P, P], U8, name="w_scales%d" % t, align_bytes=64)
            nc.vector.quantize_mx(out=codes[:].bitcast(FP8X4), scales=scales[:], in_=w_in[:])
            w_codes.append(codes)
            w_scales.append(scales)

        kept = []
        for e in range(ET):
            faded = sb.tile([P, M], F32, name="faded%d" % e, tag="k%d" % e)
            for c in range(0, M, GP_COLS):
                cols = slice(c, c + GP_COLS)
                nc.gpsimd.tensor_tensor(faded[:, cols], old_sb[e][:, cols], fade_rows[:, cols], ALU.mult)
            kept.append(faded)
        placed = [sb.tile([P, M], F32, name="placed%d" % e, tag="w%d" % e, align_bytes=64) for e in range(ET)]
        for e in range(ET):
            nc.gpsimd.memset(placed[e][:], 0.0)

        o_sb = sb.tile([P, ET, Q], F32, name="o_sb")
        for t in range(QT):
            o_bank = ps.tile([P, ET, P], F32, name="o_bank%d" % t, tag="a%d" % t)
            for e in range(ET):
                nc.tensor.matmul_mx(
                    out=o_bank[:, e, :],
                    lhsT=v_codes[e][:].bitcast(FP8X4),
                    lhsT_scale=v_scales[e][:],
                    rhs=w_codes[t][:].bitcast(FP8X4),
                    rhs_scale=w_scales[t][:],
                    start=True,
                    stop=True,
                )
            rows = slice(t * P, (t + 1) * P)
            nc.scalar.copy(o_sb[:, :, rows], o_bank[:])
            part = places[:, t * 8 : (t + 1) * 8]
            nc.vector.tensor_copy(placed[0][:].indirect(part), o_sb[:, 0, rows])
            nc.scalar.activation(placed[1][:].indirect(part), o_sb[:, 1, rows], ACT.Copy)

        for e in range(ET):
            if e >= 2:
                nc.scalar.activation(placed[e][:].indirect(places[:]), o_sb[:, e, :], ACT.Copy)
            result = sb.tile([P, M], F32, name="result%d" % e)
            pieces = 2 if e == ET - 1 else 1
            for c in range(0, M, M // pieces):
                cols = slice(c, c + M // pieces)
                nc.vector.tensor_tensor(result[:, cols], kept[e][:, cols], placed[e][:, cols], ALU.add)
                nc.sync.dma_start(out[e * P : (e + 1) * P, cols], result[:, cols])
